import numpy as np
import ml_dtypes


def mxq(x, axis, fmt="e4m3"):
    dtype, down = {"e4m3": (ml_dtypes.float8_e4m3fn, 7), "e5m2": (ml_dtypes.float8_e5m2, 14)}[fmt]
    v = np.moveaxis(np.asarray(x, np.float32).astype(ml_dtypes.bfloat16).astype(np.float64), axis, -1)
    blocks = v.reshape(v.shape[:-1] + (-1, 32))
    amax = np.abs(blocks).max(-1, keepdims=True)
    byte = np.maximum(np.where(amax > 0, np.frexp(amax)[1] - 1 + 127, 0) - down, 1)
    scale = np.exp2(byte - 127.0)
    codes = (blocks / scale).astype(np.float32).astype(dtype).astype(np.float64)
    return np.moveaxis((codes * scale).reshape(v.shape), -1, axis)


WIDE = False


def mx_kscale(k, group=512):
    if not WIDE:
        return np.ones(k)
    levels = np.array([10, -10, 5, -5, 0])
    if group != 512:
        return np.exp2(np.random.permutation(np.resize(levels, k // group))).repeat(group)
    if k % 512:
        return np.exp2(np.random.permutation(np.resize(levels, k // 32))).repeat(32)
    a = np.empty((k // 512, 16))
    for p in range(k // 512):
        a[p, :8] = np.random.permutation(np.resize(levels, 8))
        for g in range(8):
            far = levels[np.abs(levels - a[p, g]) >= 10]
            a[p, g + 8] = far[np.random.randint(len(far))]
    return np.exp2(a.ravel()).repeat(32)


def f64(x):
    return np.asarray(x).astype(np.float64)


H, D, N = 2, 256, 1024


def setup_inputs():
    n = np.random.standard_normal
    s = mx_kscale(D, 0)
    u = mx_kscale(N)
    t = np.random.uniform(0.5, 2.0, N) * u
    v = n((H, N, 128))
    v[:, :, 127] = 1.0
    return {
        "q": n((H, D, N)).astype(np.float32),
        "qa": (np.random.uniform(0.5, 2.0, D) * s)[:, None].astype(np.float32),
        "ka": np.tile(np.random.uniform(0.5, 2.0, D) / s, (128, 1)).astype(np.float32),
        "k": n((H, N, D)).astype(np.float32),
        "t": t.reshape(N, 1).astype(np.float32),
        "v": (v / t[:, None]).astype(np.float32),
        "og": n((H, N, 128)).astype(np.float32),
    }


def reference(q, qa, ka, k, t, v, og):
    fq = (np.square(f64(q)) + 0.125) * f64(qa)
    fk = (np.square(f64(k)) + 0.125) * f64(t) * f64(ka)[:1]
    S = (mxq(fk, 1, "e4m3").transpose(0, 2, 1) @ mxq(f64(v), 1, "e4m3")) / N
    y = mxq(fq, 1, "e4m3").transpose(0, 2, 1) @ mxq(S, 1, "e4m3")
    y = y / y[:, :, 127:128]
    y = y / (1.0 + np.exp(-f64(og)))
    return y

@@ -1,0 +1,247 @@
+from contextlib import ExitStack
+
+import concourse.mybir as mybir
+
+H, D, N, E = 2, 256, 1024, 128
+FLOPS = 2 * 2 * H * D * N * E
+
+F32 = mybir.dt.float32
+BF16 = mybir.dt.bfloat16
+U32 = mybir.dt.uint32
+U8 = mybir.dt.uint8
+FP8X4 = mybir.dt.float8_e4m3fn_x4
+ACT = mybir.ActivationFunctionType
+ALU = mybir.AluOpType
+P = 128
+
+ORDER = """warm: Lt: Lka: Lk:00a Lk:00b Lqa: Lk:01 Lv:0 Lk:10 Lk:11 Lq:00 Lv:1 Lq:01 Lq:10 Lq:11 Log:00 Log:01 Log:10 Log:11
+tka:0 sk:00a B:00a sk:00b B:00b tka:1 F:00 sk:01 B:01 cv:00A cv:01A rep: F:01 Fv:0 mS:0 sk:10 B:10 sk:11 F:10 B:11 cv:10V F:11 cv:11V
+sq:00 D:00 Fv:1 mS:1 S:0A sq:01 D:01 sq:10 S:1A D:10 Fq:0 FS: my:0 sq:11 D:11 r:00 r:01 Fq:1 my:1 g:00 g:01 g:10 g:11
+H:00 st:00 H:01 st:01 r:10 r:11 H:10 st:10 H:11 st:11""".split()
+
+
+def tile_rows_lin_sq_norm_gate_kernel(tc, q, qa, ka, k, t, v, og, out):
+    nc = tc.nc
+    with ExitStack() as ctx:
+        sb = ctx.enter_context(tc.tile_pool(name="sb", bufs=1))
+        ps = ctx.enter_context(tc.psum_pool(name="ps", bufs=1))
+        ctx.enter_context(tc.manual_schedule())
+
+        def tl(name, shape, dt):
+            return sb.tile(shape, dt, name=name, align_bytes=64)
+
+        warm = tl("warm", [P, 8], F32)
+        warm2 = tl("warm2", [P, 8], F32)
+        t_sb = tl("t_sb", [P, 2, 8], F32)
+        qa_sb = tl("qa_sb", [P, 8], F32)
+        qa_rep = tl("qa_rep", [P, 64, 4], F32)
+        ka_sb = tl("ka_sb", [P, D], F32)
+        tka = [tl("tka%d" % g, [P, 4, 64, 4], F32) for g in range(2)]
+        k_bf = {(h, g): tl("kbf%d%d" % (h, g), [P, 4, 64, 4], BF16) for h in range(2) for g in range(2)}
+        v_raw = [tl("vraw%d" % h, [P, 2, 4, E], F32) for h in range(2)]
+        v_bf = [tl("vbf%d" % h, [P, 2, E, 4], BF16) for h in range(2)]
+        kv_codes = [tl("kvc%d" % h, [P, 768], U32) for h in range(2)]
+        kv_scales = [tl("kvs%d" % h, [P, 768], U8) for h in range(2)]
+        K0 = [0, 256]
+        V0 = [512, 0]
+        q_bf = [tl("qbf%d" % c, [P, 4, 128, 4], BF16) for c in range(2)]
+        q_codes = [tl("qc%d" % c, [P, 512], U32) for c in range(2)]
+        q_scales = [tl("qs%d" % c, [P, 512], U8) for c in range(2)]
+        s_bf = tl("s_bf", [P, E, 4], BF16)
+        s_codes = tl("s_codes", [P, E], U32)
+        s_scales = tl("s_scales", [P, E], U8)
+        og_raw = {(c, h): tl("og%d%d" % (c, h), [P, 4, E], F32) for c in range(2) for h in range(2)}
+        gate = {(c, h): tl("gate%d%d" % (c, h), [P, 4, E], F32) for c in range(2) for h in range(2)}
+        res = {(c, h): tl("res%d%d" % (c, h), [P, 4, E], F32) for c in range(2) for h in range(2)}
+        rec = {(c, h): tl("rec%d%d" % (c, h), [P, 8], F32) for c in range(2) for h in range(2)}
+        s_ps = [ps.tile([P, 4, E], F32, name="sps%d" % h) for h in range(2)]
+        y_ps = {(c, h): ps.tile([P, 4, E], F32, name="yps%d%d" % (c, h)) for c in range(2) for h in range(2)}
+
+        k_raw, k_sq, q_raw, q_sq = {}, {}, {}, {}
+        q_rows = q.rearrange("h (p j) n -> (h p) j n", j=4)
+
+        def pp_range(part):
+            return {"a": (0, 32), "b": (32, 64), "": (0, 64)}[part]
+
+        def load_k(h, g, part):
+            a, b = pp_range(part)
+            k_raw[h, g, part] = tl("kraw%d%d%s" % (h, g, part), [P, 4, 4 * (b - a)], F32)
+            src = k[h, 512 * g : 512 * (g + 1), 4 * a : 4 * b].rearrange("(p j) d -> p j d", j=4)
+            nc.sync.dma_start(out=k_raw[h, g, part][:], in_=src)
+
+        def square_k(h, g, part):
+            a, b = pp_range(part)
+            k_sq[h, g, part] = tl("ksq%d%d%s" % (h, g, part), [P, 4, b - a, 4], F32)
+            nc.scalar.activation(
+                out=k_sq[h, g, part][:].rearrange("p x m j -> p m j x"),
+                in_=k_raw[h, g, part][:].rearrange("p j (m x) -> p m j x", x=4),
+                func=ACT.Square,
+            )
+
+        def weigh_k(h, g, part):
+            a, b = pp_range(part)
+            nc.vector.scalar_tensor_tensor(
+                out=k_bf[h, g][:, :, a:b, :], in0=k_sq[h, g, part][:], scalar=0.125,
+                in1=tka[g][:, :, a:b, :], op0=ALU.add, op1=ALU.mult,
+            )
+
+        def quant(codes, scales, src):
+            nc.vector.quantize_mx(out=codes.bitcast(FP8X4), scales=scales, in_=src)
+
+        def quant_k(h, g):
+            cols = slice(K0[h] + 256 * g, K0[h] + 256 * (g + 1))
+            quant(kv_codes[h][:, cols], kv_scales[h][:, cols], k_bf[h, g][:].rearrange("p x m j -> p (x m j)"))
+
+        def make_tka(g):
+            nc.vector.tensor_tensor(
+                out=tka[g][:],
+                in0=ka_sb[:].rearrange("p (m x) -> p x m", x=4).unsqueeze(3).to_broadcast([P, 4, 64, 4]),
+                in1=t_sb[:, g, 0:4].unsqueeze(1).unsqueeze(1).to_broadcast([P, 4, 64, 4]),
+                op=ALU.mult,
+            )
+
+        def load_v(h):
+            nc.sync.dma_start(
+                out=v_raw[h][:].rearrange("p g j e -> p g (j e)"),
+                in_=v[h].rearrange("(g p j) e -> p g (j e)", g=2, j=4),
+            )
+
+        def cast_v(h, g, eng):
+            dst = v_bf[h][:, g, :, :].rearrange("p (c i) j -> p c j i", i=4)
+            src = v_raw[h][:, g, :, :].rearrange("p j (c i) -> p c j i", i=4)
+            if eng == "A":
+                nc.scalar.activation(out=dst, in_=src, func=ACT.Copy)
+            else:
+                nc.vector.tensor_copy(out=dst, in_=src)
+
+        def quant_v(h):
+            cols = slice(V0[h], V0[h] + 256)
+            quant(kv_codes[h][:, cols], kv_scales[h][:, cols], v_bf[h][:].rearrange("p g e j -> p (g e j)"))
+
+        def state_matmuls(h):
+            for x in range(4):
+                for g in range(2):
+                    w0 = K0[h] + 256 * g + 64 * x - 64 * h
+                    w = slice(w0, w0 + 128)
+                    m = slice(V0[h] + 128 * g, V0[h] + 128 * (g + 1))
+                    nc.tensor.matmul_mx(
+                        out=s_ps[h][:, x, :],
+                        lhsT=kv_codes[h][:, w].bitcast(FP8X4), lhsT_scale=kv_scales[h][:, w],
+                        rhs=kv_codes[h][:, m].bitcast(FP8X4), rhs_scale=kv_scales[h][:, m],
+                        start=(g == 0), stop=(g == 1),
+                    )
+
+        def state_out(h, eng):
+            rows = slice(64 * h, 64 * h + 64)
+            src = s_ps[h][rows, :, :].rearrange("p x e -> p e x")
+            if eng == "A":
+                nc.scalar.activation(out=s_bf[rows, :, :], in_=src, func=ACT.Copy, scale=1.0 / N)
+            else:
+                nc.vector.tensor_scalar(out=s_bf[rows, :, :], in0=src, scalar1=1.0 / N, scalar2=None, op0=ALU.mult)
+
+        def load_q(c, f):
+            q_raw[c, f] = tl("qraw%d%d" % (c, f), [P, 4, 256], F32)
+            n0 = 512 * c + 256 * f
+            nc.sync.dma_start(out=q_raw[c, f][:], in_=q_rows[:, :, n0 : n0 + 256])
+
+        def square_q(c, f):
+            q_sq[c, f] = tl("qsq%d%d" % (c, f), [P, 4, 64, 4], F32)
+            nc.scalar.activation(
+                out=q_sq[c, f][:].rearrange("p r s j -> p s j r"),
+                in_=q_raw[c, f][:].rearrange("p j (s r) -> p s j r", r=4),
+                func=ACT.Square,
+            )
+
+        def weigh_q(c, f):
+            nc.vector.scalar_tensor_tensor(
+                out=q_bf[c][:, :, 64 * f : 64 * f + 64, :], in0=q_sq[c, f][:], scalar=0.125,
+                in1=qa_rep[:].unsqueeze(1).to_broadcast([P, 4, 64, 4]),
+                op0=ALU.add, op1=ALU.mult,
+            )
+
+        def read_matmuls(c):
+            for r in range(4):
+                for h in range(2):
+                    rows = slice(64 * h, 64 * h + 64)
+                    w = slice(128 * r, 128 * r + 128)
+                    nc.tensor.matmul_mx(
+                        out=y_ps[c, h][:, r, :],
+                        lhsT=q_codes[c][rows, w].bitcast(FP8X4), lhsT_scale=q_scales[c][rows, w],
+                        rhs=s_codes[rows, :].bitcast(FP8X4), rhs_scale=s_scales[rows, :],
+                        start=True, stop=True,
+                    )
+
+        def rows_of(x, c, h):
+            return x[h, 512 * c : 512 * (c + 1), :].rearrange("(s r) e -> s r e", r=4)
+
+        def finish(c, h, rs):
+            for r in rs:
+                nc.vector.scalar_tensor_tensor(
+                    out=res[c, h][:, r, :], in0=y_ps[c, h][:, r, :], scalar=rec[c, h][:, r : r + 1],
+                    in1=gate[c, h][:, r, :], op0=ALU.mult, op1=ALU.mult,
+                )
+
+        def step(name):
+            op, arg = name.split(":")
+            a = [int(ch) for ch in arg if ch in "0123456789"]
+            part = "".join([ch for ch in arg if ch not in "0123456789"])
+            if op == "warm":
+                nc.gpsimd.memset(warm[:], 0.0)
+                nc.scalar.activation(out=warm2[:], in_=warm[:], func=ACT.Sigmoid)
+            elif op == "Lt":
+                nc.sync.dma_start(out=t_sb[:, :, 0:4], in_=t.rearrange("(g p j) o -> p g (j o)", g=2, j=4))
+            elif op == "Lka":
+                nc.sync.dma_start(out=ka_sb[:], in_=ka)
+            elif op == "Lqa":
+                for h in range(2):
+                    nc.sync.dma_start(out=qa_sb[64 * h : 64 * h + 64, 0:4], in_=qa.rearrange("(p j) o -> p (j o)", j=4))
+            elif op == "rep":
+                nc.vector.tensor_copy(out=qa_rep[:], in_=qa_sb[:, 0:4].unsqueeze(1).to_broadcast([P, 64, 4]))
+            elif op == "Lk":
+                load_k(a[0], a[1], part)
+            elif op == "sk":
+                square_k(a[0], a[1], part)
+            elif op == "B":
+                weigh_k(a[0], a[1], part)
+            elif op == "F":
+                quant_k(a[0], a[1])
+            elif op == "tka":
+                make_tka(a[0])
+            elif op == "Lv":
+                load_v(a[0])
+            elif op == "cv":
+                cast_v(a[0], a[1], part)
+            elif op == "Fv":
+                quant_v(a[0])
+            elif op == "mS":
+                state_matmuls(a[0])
+            elif op == "S":
+                state_out(a[0], part)
+            elif op == "FS":
+                quant(s_codes[:], s_scales[:], s_bf[:].rearrange("p e x -> p (e x)"))
+            elif op == "Lq":
+                load_q(a[0], a[1])
+            elif op == "sq":
+                square_q(a[0], a[1])
+            elif op == "D":
+                weigh_q(a[0], a[1])
+            elif op == "Fq":
+                quant(q_codes[a[0]][:], q_scales[a[0]][:], q_bf[a[0]][:].rearrange("p r s j -> p (r s j)"))
+            elif op == "my":
+                read_matmuls(a[0])
+            elif op == "Log":
+                nc.sync.dma_start(out=og_raw[a[0], a[1]][:], in_=rows_of(og, a[0], a[1]))
+            elif op == "g":
+                nc.scalar.activation(out=gate[a[0], a[1]][:], in_=og_raw[a[0], a[1]][:], func=ACT.Sigmoid)
+            elif op == "r":
+                nc.vector.reciprocal(out=rec[a[0], a[1]][:, 0:4], in_=y_ps[a[0], a[1]][:, :, 127])
+            elif op == "H":
+                finish(a[0], a[1], a[2:] if len(a) > 2 else [0, 1, 2, 3])
+            elif op == "st":
+                r0, r1 = (a[2], a[3]) if len(a) > 2 else (0, 4)
+                nc.sync.dma_start(out=rows_of(out, a[0], a[1])[:, r0:r1, :], in_=res[a[0], a[1]][:, r0:r1, :])
+            else:
+                raise ValueError(name)
+
+        for name in ORDER:
+            step(name)

@@ -14,10 +14,8 @@ ACT = mybir.ActivationFunctionType
 ALU = mybir.AluOpType
 P = 128
 
-ORDER = """warm: Lt: Lka: Lk:00a Lk:00b Lqa: Lk:01 Lv:0 Lk:10 Lk:11 Lq:00 Lv:1 Lq:01 Lq:10 Lq:11 Log:00 Log:01 Log:10 Log:11
-tka:0 sk:00a B:00a sk:00b B:00b tka:1 F:00 sk:01 B:01 cv:00A cv:01A rep: F:01 Fv:0 mS:0 sk:10 B:10 sk:11 F:10 B:11 cv:10V F:11 cv:11V
-sq:00 D:00 Fv:1 mS:1 S:0A sq:01 D:01 sq:10 S:1A D:10 Fq:0 FS: my:0 sq:11 D:11 r:00 r:01 Fq:1 my:1 g:00 g:01 g:10 g:11
-H:00 st:00 H:01 st:01 r:10 r:11 H:10 st:10 H:11 st:11""".split()
+GROUPS = ["01","2","3"]
+ORDER = """warm: Lt: Lka: Lk:00 Lk:01 Lv:01 Lv:00 Lk:10 Lv:10 Lk:11 Lv:11 Lq:00 Lqa: Lq:01 Lq:10 Lq:11 Log:0 Log:1 Log:2 Log:3 sk:00a sk:00b sk:01 cv:00A sk:10 sk:11 tka:0 tka:1 B:00a cv:01V B:00b B:01 F:00 Fv:0 F:01 cv:10V B:10 cv:11V F:10 B:11 Fv:1 F:11 mS:0 mS:1 S:0A sq:0 sq:1 S:1A sq:2 sq:3 g:0 g:1 g:2 g:3 D:0 D:1 FS: Fq:01 D:2 my:01 r:010 r:011 Fq:2 D:3 H:00 st:00 Fq:3 H:01 st:01 my:2 my:3 r:20 r:21 H:10 st:10 H:11 st:11 r:30 r:31 H:20 st:20 H:21 st:21 H:30 st:30 H:31 st:31""".split()
 
 
 def tile_rows_lin_sq_norm_gate_kernel(tc, q, qa, ka, k, t, v, og, out):
@@ -34,7 +32,6 @@ def tile_rows_lin_sq_norm_gate_kernel(tc, q, qa, ka, k, t, v, og, out):
         warm2 = tl("warm2", [P, 8], F32)
         t_sb = tl("t_sb", [P, 2, 8], F32)
         qa_sb = tl("qa_sb", [P, 8], F32)
-        qa_rep = tl("qa_rep", [P, 64, 4], F32)
         ka_sb = tl("ka_sb", [P, D], F32)
         tka = [tl("tka%d" % g, [P, 4, 64, 4], F32) for g in range(2)]
         k_bf = {(h, g): tl("kbf%d%d" % (h, g), [P, 4, 64, 4], BF16) for h in range(2) for g in range(2)}
@@ -44,18 +41,23 @@ def tile_rows_lin_sq_norm_gate_kernel(tc, q, qa, ka, k, t, v, og, out):
         kv_scales = [tl("kvs%d" % h, [P, 768], U8) for h in range(2)]
         K0 = [0, 256]
         V0 = [512, 0]
-        q_bf = [tl("qbf%d" % c, [P, 4, 128, 4], BF16) for c in range(2)]
-        q_codes = [tl("qc%d" % c, [P, 512], U32) for c in range(2)]
-        q_scales = [tl("qs%d" % c, [P, 512], U8) for c in range(2)]
+        q_bf = {G: tl("qbf" + G, [P, len(G), 256, 4], BF16) for G in GROUPS}
+        q_codes = {G: tl("qc" + G, [P, 256 * len(G)], U32) for G in GROUPS}
+        q_scales = {G: tl("qs" + G, [P, 256 * len(G)], U8) for G in GROUPS}
+        group_of = {int(u): G for G in GROUPS for u in G}
         s_bf = tl("s_bf", [P, E, 4], BF16)
         s_codes = tl("s_codes", [P, E], U32)
         s_scales = tl("s_scales", [P, E], U8)
-        og_raw = {(c, h): tl("og%d%d" % (c, h), [P, 4, E], F32) for c in range(2) for h in range(2)}
-        gate = {(c, h): tl("gate%d%d" % (c, h), [P, 4, E], F32) for c in range(2) for h in range(2)}
-        res = {(c, h): tl("res%d%d" % (c, h), [P, 4, E], F32) for c in range(2) for h in range(2)}
-        rec = {(c, h): tl("rec%d%d" % (c, h), [P, 8], F32) for c in range(2) for h in range(2)}
+        og_raw = [tl("og%d" % u, [P, 2, 2, E], F32) for u in range(4)]
+        gate = [tl("gate%d" % u, [P, 2, 2, E], F32) for u in range(4)]
+        res = [tl("res%d" % u, [P, 2, 2, E], F32) for u in range(4)]
+        rec = {(G, h): tl("rec%s%d" % (G, h), [P, 8], F32) for G in GROUPS for h in range(2)}
         s_ps = [ps.tile([P, 4, E], F32, name="sps%d" % h) for h in range(2)]
-        y_ps = {(c, h): ps.tile([P, 4, E], F32, name="yps%d%d" % (c, h)) for c in range(2) for h in range(2)}
+        y_bank = {(b, h): ps.tile([P, 4, E], F32, name="yps%d%d" % (b, h)) for b in range(min(3, len(GROUPS))) for h in range(2)}
+        y_ps = {}
+        for i, G in enumerate(GROUPS):
+            for h in range(2):
+                y_ps[G, h] = y_bank[i % 3, h][:, 2 * (i // 3) : 2 * (i // 3) + 2 * len(G), :]
 
         k_raw, k_sq, q_raw, q_sq = {}, {}, {}, {}
         q_rows = q.rearrange("h (p j) n -> (h p) j n", j=4)
@@ -74,7 +76,7 @@ def tile_rows_lin_sq_norm_gate_kernel(tc, q, qa, ka, k, t, v, og, out):
             k_sq[h, g, part] = tl("ksq%d%d%s" % (h, g, part), [P, 4, b - a, 4], F32)
             nc.scalar.activation(
                 out=k_sq[h, g, part][:].rearrange("p x m j -> p m j x"),
-                in_=k_raw[h, g, part][:].rearrange("p j (m x) -> p m j x", x=4),
+                in_=(k_raw[h, g, part][:] if (h, g, part) in k_raw else k_raw[h, g, ""][:, :, 4 * a : 4 * b]).rearrange("p j (m x) -> p m j x", x=4),
                 func=ACT.Square,
             )
 
@@ -100,10 +102,10 @@ def tile_rows_lin_sq_norm_gate_kernel(tc, q, qa, ka, k, t, v, og, out):
                 op=ALU.mult,
             )
 
-        def load_v(h):
+        def load_v(h, g):
             nc.sync.dma_start(
-                out=v_raw[h][:].rearrange("p g j e -> p g (j e)"),
-                in_=v[h].rearrange("(g p j) e -> p g (j e)", g=2, j=4),
+                out=v_raw[h][:, g, :, :],
+                in_=v[h, 512 * g : 512 * (g + 1), :].rearrange("(p j) e -> p j e", j=4),
             )
 
         def cast_v(h, g, eng):
@@ -139,46 +141,51 @@ def tile_rows_lin_sq_norm_gate_kernel(tc, q, qa, ka, k, t, v, og, out):
             else:
                 nc.vector.tensor_scalar(out=s_bf[rows, :, :], in0=src, scalar1=1.0 / N, scalar2=None, op0=ALU.mult)
 
-        def load_q(c, f):
-            q_raw[c, f] = tl("qraw%d%d" % (c, f), [P, 4, 256], F32)
-            n0 = 512 * c + 256 * f
-            nc.sync.dma_start(out=q_raw[c, f][:], in_=q_rows[:, :, n0 : n0 + 256])
+        def load_q(a):
+            n0, w = (512 * a[0], 512) if len(a) == 1 else (512 * a[0] + 256 * a[1], 256)
+            raw = tl("qraw%d" % n0, [P, 4, w], F32)
+            nc.sync.dma_start(out=raw[:], in_=q_rows[:, :, n0 : n0 + w])
+            for i in range(w // 256):
+                q_raw[n0 // 256 + i] = raw[:, :, 256 * i : 256 * (i + 1)]
 
-        def square_q(c, f):
-            q_sq[c, f] = tl("qsq%d%d" % (c, f), [P, 4, 64, 4], F32)
+        def square_q(u):
+            q_sq[u] = tl("qsq%d" % u, [P, 2, 128, 4], F32)
             nc.scalar.activation(
-                out=q_sq[c, f][:].rearrange("p r s j -> p s j r"),
-                in_=q_raw[c, f][:].rearrange("p j (s r) -> p s j r", r=4),
+                out=q_sq[u][:].rearrange("p r s j -> p s j r"),
+                in_=q_raw[u].rearrange("p j (s r) -> p s j r", r=2),
                 func=ACT.Square,
             )
 
-        def weigh_q(c, f):
+        def weigh_q(u):
+            G = group_of[u]
             nc.vector.scalar_tensor_tensor(
-                out=q_bf[c][:, :, 64 * f : 64 * f + 64, :], in0=q_sq[c, f][:], scalar=0.125,
-                in1=qa_rep[:].unsqueeze(1).to_broadcast([P, 4, 64, 4]),
+                out=q_bf[G][:, G.index(str(u)), :, :], in0=q_sq[u][:].rearrange("p r s j -> p (r s) j"), scalar=0.125,
+                in1=qa_sb[:, 0:4].unsqueeze(1).to_broadcast([P, 256, 4]),
                 op0=ALU.add, op1=ALU.mult,
             )
 
-        def read_matmuls(c):
-            for r in range(4):
+        def read_matmuls(G):
+            for r in range(2 * len(G)):
                 for h in range(2):
                     rows = slice(64 * h, 64 * h + 64)
                     w = slice(128 * r, 128 * r + 128)
                     nc.tensor.matmul_mx(
-                        out=y_ps[c, h][:, r, :],
-                        lhsT=q_codes[c][rows, w].bitcast(FP8X4), lhsT_scale=q_scales[c][rows, w],
+                        out=y_ps[G, h][:, r, :],
+                        lhsT=q_codes[G][rows, w].bitcast(FP8X4), lhsT_scale=q_scales[G][rows, w],
                         rhs=s_codes[rows, :].bitcast(FP8X4), rhs_scale=s_scales[rows, :],
                         start=True, stop=True,
                     )
 
-        def rows_of(x, c, h):
-            return x[h, 512 * c : 512 * (c + 1), :].rearrange("(s r) e -> s r e", r=4)
+        def rows_of(x, u):
+            return x[:, 256 * u : 256 * (u + 1), :].rearrange("h (s r) e -> s h r e", r=2)
 
-        def finish(c, h, rs):
-            for r in rs:
+        def finish(u, h):
+            G = group_of[u]
+            for r in range(2):
+                i = 2 * G.index(str(u)) + r
                 nc.vector.scalar_tensor_tensor(
-                    out=res[c, h][:, r, :], in0=y_ps[c, h][:, r, :], scalar=rec[c, h][:, r : r + 1],
-                    in1=gate[c, h][:, r, :], op0=ALU.mult, op1=ALU.mult,
+                    out=res[u][:, h, r, :], in0=y_ps[G, h][:, i, :], scalar=rec[G, h][:, i : i + 1],
+                    in1=gate[u][:, h, r, :], op0=ALU.mult, op1=ALU.mult,
                 )
 
         def step(name):
@@ -195,8 +202,6 @@ def tile_rows_lin_sq_norm_gate_kernel(tc, q, qa, ka, k, t, v, og, out):
             elif op == "Lqa":
                 for h in range(2):
                     nc.sync.dma_start(out=qa_sb[64 * h : 64 * h + 64, 0:4], in_=qa.rearrange("(p j) o -> p (j o)", j=4))
-            elif op == "rep":
-                nc.vector.tensor_copy(out=qa_rep[:], in_=qa_sb[:, 0:4].unsqueeze(1).to_broadcast([P, 64, 4]))
             elif op == "Lk":
                 load_k(a[0], a[1], part)
             elif op == "sk":
@@ -208,7 +213,7 @@ def tile_rows_lin_sq_norm_gate_kernel(tc, q, qa, ka, k, t, v, og, out):
             elif op == "tka":
                 make_tka(a[0])
             elif op == "Lv":
-                load_v(a[0])
+                load_v(a[0], a[1])
             elif op == "cv":
                 cast_v(a[0], a[1], part)
             elif op == "Fv":
@@ -220,26 +225,27 @@ def tile_rows_lin_sq_norm_gate_kernel(tc, q, qa, ka, k, t, v, og, out):
             elif op == "FS":
                 quant(s_codes[:], s_scales[:], s_bf[:].rearrange("p e x -> p (e x)"))
             elif op == "Lq":
-                load_q(a[0], a[1])
+                load_q(a)
             elif op == "sq":
-                square_q(a[0], a[1])
+                square_q(a[0])
             elif op == "D":
-                weigh_q(a[0], a[1])
+                weigh_q(a[0])
             elif op == "Fq":
-                quant(q_codes[a[0]][:], q_scales[a[0]][:], q_bf[a[0]][:].rearrange("p r s j -> p (r s j)"))
+                quant(q_codes[arg][:], q_scales[arg][:], q_bf[arg][:].rearrange("p u s j -> p (u s j)"))
             elif op == "my":
-                read_matmuls(a[0])
+                read_matmuls(arg)
             elif op == "Log":
-                nc.sync.dma_start(out=og_raw[a[0], a[1]][:], in_=rows_of(og, a[0], a[1]))
+                nc.sync.dma_start(out=og_raw[a[0]][:], in_=rows_of(og, a[0]))
             elif op == "g":
-                nc.scalar.activation(out=gate[a[0], a[1]][:], in_=og_raw[a[0], a[1]][:], func=ACT.Sigmoid)
+                nc.scalar.activation(out=gate[a[0]][:], in_=og_raw[a[0]][:], func=ACT.Sigmoid)
             elif op == "r":
-                nc.vector.reciprocal(out=rec[a[0], a[1]][:, 0:4], in_=y_ps[a[0], a[1]][:, :, 127])
+                G = arg[:-1]
+                nc.vector.reciprocal(out=rec[G, a[-1]][:, 0 : 2 * len(G)], in_=y_ps[G, a[-1]][:, :, 127])
             elif op == "H":
-                finish(a[0], a[1], a[2:] if len(a) > 2 else [0, 1, 2, 3])
+                finish(a[0], a[1])
             elif op == "st":
-                r0, r1 = (a[2], a[3]) if len(a) > 2 else (0, 4)
-                nc.sync.dma_start(out=rows_of(out, a[0], a[1])[:, r0:r1, :], in_=res[a[0], a[1]][:, r0:r1, :])
+                h0, h1 = (a[1], a[1] + 1) if len(a) > 1 else (0, 2)
+                nc.sync.dma_start(out=rows_of(out, a[0])[:, h0:h1, :, :], in_=res[a[0]][:, h0:h1, :, :])
             else:
                 raise ValueError(name)
 

@@ -15,7 +15,7 @@ ALU = mybir.AluOpType
 P = 128
 
 GROUPS = ["01","2","3"]
-ORDER = """warm: Lt: Lka: Lk:00 Lk:01 Lv:01 Lv:00 Lk:10 Lv:10 Lk:11 Lv:11 Lq:00 Lqa: Lq:01 Lq:10 Lq:11 Log:0 Log:1 Log:2 Log:3 sk:00a sk:00b sk:01 cv:00A sk:10 sk:11 tka:0 tka:1 B:00a cv:01V B:00b B:01 F:00 Fv:0 F:01 cv:10V B:10 cv:11V F:10 B:11 Fv:1 F:11 mS:0 mS:1 S:0A sq:0 sq:1 S:1A sq:2 sq:3 g:0 g:1 g:2 g:3 D:0 D:1 FS: Fq:01 D:2 my:01 r:010 r:011 Fq:2 D:3 H:00 st:00 Fq:3 H:01 st:01 my:2 my:3 r:20 r:21 H:10 st:10 H:11 st:11 r:30 r:31 H:20 st:20 H:21 st:21 H:30 st:30 H:31 st:31""".split()
+ORDER = """Lt: Lqa: warm: Lka: Lk:00 Lk:01 Lv:01 Lv:00 Lk:10 Lk:11 Lv:10 Lq:00 Lv:11 Lq:01 Lq:10 Lq:11 Log:0 Log:1 Log:2 Log:3 sk:00a sk:00b sk:01 cv:00A sk:10 sk:11 sq:0 tka:0 tka:1 B:00a B:00b cv:01V B:01 F:00 Fv:0 F:01 B:10 cv:10V B:11 cv:11V F:10 F:11 Fv:1 D:0 mS:0 mS:1 S:0A sq:1 sq:2 S:1A sq:3 g:0 g:1 g:2 g:3 D:1 Fq:0 Fq:1 D:2 FS: Fq:2 D:3 my:01 my:2 r:010 r:011 Fq:3 H:00 st:00 H:01 st:01 r:20 r:21 H:10 st:10 H:11 st:11 my:3 r:30 r:31 H:20 st:20 H:21 st:21 H:30 st:30 H:310 st:310 H:311 st:311""".split()
 
 
 def tile_rows_lin_sq_norm_gate_kernel(tc, q, qa, ka, k, t, v, og, out):
@@ -179,9 +179,9 @@ def tile_rows_lin_sq_norm_gate_kernel(tc, q, qa, ka, k, t, v, og, out):
         def rows_of(x, u):
             return x[:, 256 * u : 256 * (u + 1), :].rearrange("h (s r) e -> s h r e", r=2)
 
-        def finish(u, h):
+        def finish(u, h, rs):
             G = group_of[u]
-            for r in range(2):
+            for r in rs:
                 i = 2 * G.index(str(u)) + r
                 nc.vector.scalar_tensor_tensor(
                     out=res[u][:, h, r, :], in0=y_ps[G, h][:, i, :], scalar=rec[G, h][:, i : i + 1],
@@ -196,12 +196,12 @@ def tile_rows_lin_sq_norm_gate_kernel(tc, q, qa, ka, k, t, v, og, out):
                 nc.gpsimd.memset(warm[:], 0.0)
                 nc.scalar.activation(out=warm2[:], in_=warm[:], func=ACT.Sigmoid)
             elif op == "Lt":
-                nc.sync.dma_start(out=t_sb[:, :, 0:4], in_=t.rearrange("(g p j) o -> p g (j o)", g=2, j=4))
+                nc.scalar.dma_start(out=t_sb[:, :, 0:4], in_=t.rearrange("(g p j) o -> p g (j o)", g=2, j=4))
             elif op == "Lka":
                 nc.sync.dma_start(out=ka_sb[:], in_=ka)
             elif op == "Lqa":
                 for h in range(2):
-                    nc.sync.dma_start(out=qa_sb[64 * h : 64 * h + 64, 0:4], in_=qa.rearrange("(p j) o -> p (j o)", j=4))
+                    nc.scalar.dma_start(out=qa_sb[64 * h : 64 * h + 64, 0:4], in_=qa.rearrange("(p j) o -> p (j o)", j=4))
             elif op == "Lk":
                 load_k(a[0], a[1], part)
             elif op == "sk":
@@ -231,7 +231,10 @@ def tile_rows_lin_sq_norm_gate_kernel(tc, q, qa, ka, k, t, v, og, out):
             elif op == "D":
                 weigh_q(a[0])
             elif op == "Fq":
-                quant(q_codes[arg][:], q_scales[arg][:], q_bf[arg][:].rearrange("p u s j -> p (u s j)"))
+                G = group_of[a[0]]
+                i = G.index(arg)
+                cols = slice(256 * i, 256 * (i + 1))
+                quant(q_codes[G][:, cols], q_scales[G][:, cols], q_bf[G][:, i, :, :].rearrange("p s j -> p (s j)"))
             elif op == "my":
                 read_matmuls(arg)
             elif op == "Log":
@@ -242,10 +245,18 @@ def tile_rows_lin_sq_norm_gate_kernel(tc, q, qa, ka, k, t, v, og, out):
                 G = arg[:-1]
                 nc.vector.reciprocal(out=rec[G, a[-1]][:, 0 : 2 * len(G)], in_=y_ps[G, a[-1]][:, :, 127])
             elif op == "H":
-                finish(a[0], a[1])
+                finish(a[0], a[1], a[2:] if len(a) > 2 else [0, 1])
+            elif op == "yr":
+                G = group_of[a[0]]
+                for r in range(2):
+                    i = 2 * G.index(str(a[0])) + r
+                    nc.scalar.activation(out=og_raw[a[0]][:, a[1], r, :], in_=y_ps[G, a[1]][:, i, :], func=ACT.Copy, scale=rec[G, a[1]][:, i : i + 1])
+            elif op == "Hp":
+                nc.gpsimd.tensor_tensor(out=res[a[0]][:, a[1], :, :], in0=og_raw[a[0]][:, a[1], :, :], in1=gate[a[0]][:, a[1], :, :], op=ALU.mult)
             elif op == "st":
                 h0, h1 = (a[1], a[1] + 1) if len(a) > 1 else (0, 2)
-                nc.sync.dma_start(out=rows_of(out, a[0])[:, h0:h1, :, :], in_=res[a[0]][:, h0:h1, :, :])
+                r0, r1 = (a[2], a[2] + 1) if len(a) > 2 else (0, 2)
+                nc.sync.dma_start(out=rows_of(out, a[0])[:, h0:h1, r0:r1, :], in_=res[a[0]][:, h0:h1, r0:r1, :])
             else:
                 raise ValueError(name)
 

from contextlib import ExitStack

import concourse.mybir as mybir

H, D, N, E = 2, 256, 1024, 128
FLOPS = 2 * 2 * H * D * N * E

F32 = mybir.dt.float32
BF16 = mybir.dt.bfloat16
U32 = mybir.dt.uint32
U8 = mybir.dt.uint8
FP8X4 = mybir.dt.float8_e4m3fn_x4
ACT = mybir.ActivationFunctionType
ALU = mybir.AluOpType
P = 128

GROUPS = ["01","2","3"]
ORDER = """Lt: Lqa: warm: Lka: Lk:00 Lk:01 Lv:01 Lv:00 Lk:10 Lk:11 Lv:10 Lq:00 Lv:11 Lq:01 Lq:10 Lq:11 Log:0 Log:1 Log:2 Log:3 sk:00a sk:00b sk:01 cv:00A sk:10 sk:11 sq:0 tka:0 tka:1 B:00a B:00b cv:01V B:01 F:00 Fv:0 F:01 B:10 cv:10V B:11 cv:11V F:10 F:11 Fv:1 D:0 mS:0 mS:1 S:0A sq:1 sq:2 S:1A sq:3 g:0 g:1 g:2 g:3 D:1 Fq:0 Fq:1 D:2 FS: Fq:2 D:3 my:01 my:2 r:010 r:011 Fq:3 H:00 st:00 H:01 st:01 r:20 r:21 H:10 st:10 H:11 st:11 my:3 r:30 r:31 H:20 st:20 H:21 st:21 H:30 st:30 H:310 st:310 H:311 st:311""".split()


def tile_rows_lin_sq_norm_gate_kernel(tc, q, qa, ka, k, t, v, og, out):
    nc = tc.nc
    with ExitStack() as ctx:
        sb = ctx.enter_context(tc.tile_pool(name="sb", bufs=1))
        ps = ctx.enter_context(tc.psum_pool(name="ps", bufs=1))
        ctx.enter_context(tc.manual_schedule())

        def tl(name, shape, dt):
            return sb.tile(shape, dt, name=name, align_bytes=64)

        warm = tl("warm", [P, 8], F32)
        warm2 = tl("warm2", [P, 8], F32)
        t_sb = tl("t_sb", [P, 2, 8], F32)
        qa_sb = tl("qa_sb", [P, 8], F32)
        ka_sb = tl("ka_sb", [P, D], F32)
        tka = [tl("tka%d" % g, [P, 4, 64, 4], F32) for g in range(2)]
        k_bf = {(h, g): tl("kbf%d%d" % (h, g), [P, 4, 64, 4], BF16) for h in range(2) for g in range(2)}
        v_raw = [tl("vraw%d" % h, [P, 2, 4, E], F32) for h in range(2)]
        v_bf = [tl("vbf%d" % h, [P, 2, E, 4], BF16) for h in range(2)]
        kv_codes = [tl("kvc%d" % h, [P, 768], U32) for h in range(2)]
        kv_scales = [tl("kvs%d" % h, [P, 768], U8) for h in range(2)]
        K0 = [0, 256]
        V0 = [512, 0]
        q_bf = {G: tl("qbf" + G, [P, len(G), 256, 4], BF16) for G in GROUPS}
        q_codes = {G: tl("qc" + G, [P, 256 * len(G)], U32) for G in GROUPS}
        q_scales = {G: tl("qs" + G, [P, 256 * len(G)], U8) for G in GROUPS}
        group_of = {int(u): G for G in GROUPS for u in G}
        s_bf = tl("s_bf", [P, E, 4], BF16)
        s_codes = tl("s_codes", [P, E], U32)
        s_scales = tl("s_scales", [P, E], U8)
        og_raw = [tl("og%d" % u, [P, 2, 2, E], F32) for u in range(4)]
        gate = [tl("gate%d" % u, [P, 2, 2, E], F32) for u in range(4)]
        res = [tl("res%d" % u, [P, 2, 2, E], F32) for u in range(4)]
        rec = {(G, h): tl("rec%s%d" % (G, h), [P, 8], F32) for G in GROUPS for h in range(2)}
        s_ps = [ps.tile([P, 4, E], F32, name="sps%d" % h) for h in range(2)]
        y_bank = {(b, h): ps.tile([P, 4, E], F32, name="yps%d%d" % (b, h)) for b in range(min(3, len(GROUPS))) for h in range(2)}
        y_ps = {}
        for i, G in enumerate(GROUPS):
            for h in range(2):
                y_ps[G, h] = y_bank[i % 3, h][:, 2 * (i // 3) : 2 * (i // 3) + 2 * len(G), :]

        k_raw, k_sq, q_raw, q_sq = {}, {}, {}, {}
        q_rows = q.rearrange("h (p j) n -> (h p) j n", j=4)

        def pp_range(part):
            return {"a": (0, 32), "b": (32, 64), "": (0, 64)}[part]

        def load_k(h, g, part):
            a, b = pp_range(part)
            k_raw[h, g, part] = tl("kraw%d%d%s" % (h, g, part), [P, 4, 4 * (b - a)], F32)
            src = k[h, 512 * g : 512 * (g + 1), 4 * a : 4 * b].rearrange("(p j) d -> p j d", j=4)
            nc.sync.dma_start(out=k_raw[h, g, part][:], in_=src)

        def square_k(h, g, part):
            a, b = pp_range(part)
            k_sq[h, g, part] = tl("ksq%d%d%s" % (h, g, part), [P, 4, b - a, 4], F32)
            nc.scalar.activation(
                out=k_sq[h, g, part][:].rearrange("p x m j -> p m j x"),
                in_=(k_raw[h, g, part][:] if (h, g, part) in k_raw else k_raw[h, g, ""][:, :, 4 * a : 4 * b]).rearrange("p j (m x) -> p m j x", x=4),
                func=ACT.Square,
            )

        def weigh_k(h, g, part):
            a, b = pp_range(part)
            nc.vector.scalar_tensor_tensor(
                out=k_bf[h, g][:, :, a:b, :], in0=k_sq[h, g, part][:], scalar=0.125,
                in1=tka[g][:, :, a:b, :], op0=ALU.add, op1=ALU.mult,
            )

        def quant(codes, scales, src):
            nc.vector.quantize_mx(out=codes.bitcast(FP8X4), scales=scales, in_=src)

        def quant_k(h, g):
            cols = slice(K0[h] + 256 * g, K0[h] + 256 * (g + 1))
            quant(kv_codes[h][:, cols], kv_scales[h][:, cols], k_bf[h, g][:].rearrange("p x m j -> p (x m j)"))

        def make_tka(g):
            nc.vector.tensor_tensor(
                out=tka[g][:],
                in0=ka_sb[:].rearrange("p (m x) -> p x m", x=4).unsqueeze(3).to_broadcast([P, 4, 64, 4]),
                in1=t_sb[:, g, 0:4].unsqueeze(1).unsqueeze(1).to_broadcast([P, 4, 64, 4]),
                op=ALU.mult,
            )

        def load_v(h, g):
            nc.sync.dma_start(
                out=v_raw[h][:, g, :, :],
                in_=v[h, 512 * g : 512 * (g + 1), :].rearrange("(p j) e -> p j e", j=4),
            )

        def cast_v(h, g, eng):
            dst = v_bf[h][:, g, :, :].rearrange("p (c i) j -> p c j i", i=4)
            src = v_raw[h][:, g, :, :].rearrange("p j (c i) -> p c j i", i=4)
            if eng == "A":
                nc.scalar.activation(out=dst, in_=src, func=ACT.Copy)
            else:
                nc.vector.tensor_copy(out=dst, in_=src)

        def quant_v(h):
            cols = slice(V0[h], V0[h] + 256)
            quant(kv_codes[h][:, cols], kv_scales[h][:, cols], v_bf[h][:].rearrange("p g e j -> p (g e j)"))

        def state_matmuls(h):
            for x in range(4):
                for g in range(2):
                    w0 = K0[h] + 256 * g + 64 * x - 64 * h
                    w = slice(w0, w0 + 128)
                    m = slice(V0[h] + 128 * g, V0[h] + 128 * (g + 1))
                    nc.tensor.matmul_mx(
                        out=s_ps[h][:, x, :],
                        lhsT=kv_codes[h][:, w].bitcast(FP8X4), lhsT_scale=kv_scales[h][:, w],
                        rhs=kv_codes[h][:, m].bitcast(FP8X4), rhs_scale=kv_scales[h][:, m],
                        start=(g == 0), stop=(g == 1),
                    )

        def state_out(h, eng):
            rows = slice(64 * h, 64 * h + 64)
            src = s_ps[h][rows, :, :].rearrange("p x e -> p e x")
            if eng == "A":
                nc.scalar.activation(out=s_bf[rows, :, :], in_=src, func=ACT.Copy, scale=1.0 / N)
            else:
                nc.vector.tensor_scalar(out=s_bf[rows, :, :], in0=src, scalar1=1.0 / N, scalar2=None, op0=ALU.mult)

        def load_q(a):
            n0, w = (512 * a[0], 512) if len(a) == 1 else (512 * a[0] + 256 * a[1], 256)
            raw = tl("qraw%d" % n0, [P, 4, w], F32)
            nc.sync.dma_start(out=raw[:], in_=q_rows[:, :, n0 : n0 + w])
            for i in range(w // 256):
                q_raw[n0 // 256 + i] = raw[:, :, 256 * i : 256 * (i + 1)]

        def square_q(u):
            q_sq[u] = tl("qsq%d" % u, [P, 2, 128, 4], F32)
            nc.scalar.activation(
                out=q_sq[u][:].rearrange("p r s j -> p s j r"),
                in_=q_raw[u].rearrange("p j (s r) -> p s j r", r=2),
                func=ACT.Square,
            )

        def weigh_q(u):
            G = group_of[u]
            nc.vector.scalar_tensor_tensor(
                out=q_bf[G][:, G.index(str(u)), :, :], in0=q_sq[u][:].rearrange("p r s j -> p (r s) j"), scalar=0.125,
                in1=qa_sb[:, 0:4].unsqueeze(1).to_broadcast([P, 256, 4]),
                op0=ALU.add, op1=ALU.mult,
            )

        def read_matmuls(G):
            for r in range(2 * len(G)):
                for h in range(2):
                    rows = slice(64 * h, 64 * h + 64)
                    w = slice(128 * r, 128 * r + 128)
                    nc.tensor.matmul_mx(
                        out=y_ps[G, h][:, r, :],
                        lhsT=q_codes[G][rows, w].bitcast(FP8X4), lhsT_scale=q_scales[G][rows, w],
                        rhs=s_codes[rows, :].bitcast(FP8X4), rhs_scale=s_scales[rows, :],
                        start=True, stop=True,
                    )

        def rows_of(x, u):
            return x[:, 256 * u : 256 * (u + 1), :].rearrange("h (s r) e -> s h r e", r=2)

        def finish(u, h, rs):
            G = group_of[u]
            for r in rs:
                i = 2 * G.index(str(u)) + r
                nc.vector.scalar_tensor_tensor(
                    out=res[u][:, h, r, :], in0=y_ps[G, h][:, i, :], scalar=rec[G, h][:, i : i + 1],
                    in1=gate[u][:, h, r, :], op0=ALU.mult, op1=ALU.mult,
                )

        def step(name):
            op, arg = name.split(":")
            a = [int(ch) for ch in arg if ch in "0123456789"]
            part = "".join([ch for ch in arg if ch not in "0123456789"])
            if op == "warm":
                nc.gpsimd.memset(warm[:], 0.0)
                nc.scalar.activation(out=warm2[:], in_=warm[:], func=ACT.Sigmoid)
            elif op == "Lt":
                nc.scalar.dma_start(out=t_sb[:, :, 0:4], in_=t.rearrange("(g p j) o -> p g (j o)", g=2, j=4))
            elif op == "Lka":
                nc.sync.dma_start(out=ka_sb[:], in_=ka)
            elif op == "Lqa":
                for h in range(2):
                    nc.scalar.dma_start(out=qa_sb[64 * h : 64 * h + 64, 0:4], in_=qa.rearrange("(p j) o -> p (j o)", j=4))
            elif op == "Lk":
                load_k(a[0], a[1], part)
            elif op == "sk":
                square_k(a[0], a[1], part)
            elif op == "B":
                weigh_k(a[0], a[1], part)
            elif op == "F":
                quant_k(a[0], a[1])
            elif op == "tka":
                make_tka(a[0])
            elif op == "Lv":
                load_v(a[0], a[1])
            elif op == "cv":
                cast_v(a[0], a[1], part)
            elif op == "Fv":
                quant_v(a[0])
            elif op == "mS":
                state_matmuls(a[0])
            elif op == "S":
                state_out(a[0], part)
            elif op == "FS":
                quant(s_codes[:], s_scales[:], s_bf[:].rearrange("p e x -> p (e x)"))
            elif op == "Lq":
                load_q(a)
            elif op == "sq":
                square_q(a[0])
            elif op == "D":
                weigh_q(a[0])
            elif op == "Fq":
                G = group_of[a[0]]
                i = G.index(arg)
                cols = slice(256 * i, 256 * (i + 1))
                quant(q_codes[G][:, cols], q_scales[G][:, cols], q_bf[G][:, i, :, :].rearrange("p s j -> p (s j)"))
            elif op == "my":
                read_matmuls(arg)
            elif op == "Log":
                nc.sync.dma_start(out=og_raw[a[0]][:], in_=rows_of(og, a[0]))
            elif op == "g":
                nc.scalar.activation(out=gate[a[0]][:], in_=og_raw[a[0]][:], func=ACT.Sigmoid)
            elif op == "r":
                G = arg[:-1]
                nc.vector.reciprocal(out=rec[G, a[-1]][:, 0 : 2 * len(G)], in_=y_ps[G, a[-1]][:, :, 127])
            elif op == "H":
                finish(a[0], a[1], a[2:] if len(a) > 2 else [0, 1])
            elif op == "yr":
                G = group_of[a[0]]
                for r in range(2):
                    i = 2 * G.index(str(a[0])) + r
                    nc.scalar.activation(out=og_raw[a[0]][:, a[1], r, :], in_=y_ps[G, a[1]][:, i, :], func=ACT.Copy, scale=rec[G, a[1]][:, i : i + 1])
            elif op == "Hp":
                nc.gpsimd.tensor_tensor(out=res[a[0]][:, a[1], :, :], in0=og_raw[a[0]][:, a[1], :, :], in1=gate[a[0]][:, a[1], :, :], op=ALU.mult)
            elif op == "st":
                h0, h1 = (a[1], a[1] + 1) if len(a) > 1 else (0, 2)
                r0, r1 = (a[2], a[2] + 1) if len(a) > 2 else (0, 2)
                nc.sync.dma_start(out=rows_of(out, a[0])[:, h0:h1, r0:r1, :], in_=res[a[0]][:, h0:h1, r0:r1, :])
            else:
                raise ValueError(name)

        for name in ORDER:
            step(name)
